import numpy as np
import ml_dtypes


def mxq(x, axis, fmt="e4m3"):
    dtype, down = {"e4m3": (ml_dtypes.float8_e4m3fn, 7), "e5m2": (ml_dtypes.float8_e5m2, 14)}[fmt]
    v = np.moveaxis(np.asarray(x, np.float32).astype(ml_dtypes.bfloat16).astype(np.float64), axis, -1)
    blocks = v.reshape(v.shape[:-1] + (-1, 32))
    amax = np.abs(blocks).max(-1, keepdims=True)
    byte = np.maximum(np.where(amax > 0, np.frexp(amax)[1] - 1 + 127, 0) - down, 1)
    scale = np.exp2(byte - 127.0)
    codes = (blocks / scale).astype(np.float32).astype(dtype).astype(np.float64)
    return np.moveaxis((codes * scale).reshape(v.shape), -1, axis)


WIDE = False


def mx_kscale(k):
    if not WIDE:
        return np.ones(k)
    levels = np.array([10, -10, 5, -5, 0])
    if k % 512:
        return np.exp2(np.random.permutation(np.resize(levels, k // 32))).repeat(32)
    a = np.empty((k // 512, 16))
    for p in range(k // 512):
        a[p, :8] = np.random.permutation(np.resize(levels, 8))
        for g in range(8):
            far = levels[np.abs(levels - a[p, g]) >= 10]
            a[p, g + 8] = far[np.random.randint(len(far))]
    return np.exp2(a.ravel()).repeat(32)


def f64(x):
    return np.asarray(x).astype(np.float64)


def striped(idx):
    return np.tile(idx.reshape(-1, 16).T, (8, 1)).astype(np.uint16)


def unstriped(offs):
    return offs[:16].T.reshape(-1).astype(np.int64)


E2M1 = np.array([0.0, 0.5, 1.0, 1.5, 2.0, 3.0, 4.0, 6.0, -0.0, -0.5, -1.0, -1.5, -2.0, -3.0, -4.0, -6.0])


def pack_weight(w, fmt):
    k, n = w.shape
    w = f64(np.asarray(w, np.float32).astype(ml_dtypes.bfloat16)).reshape(k // 32, 32, n)
    amax = np.abs(w).max(1)
    if fmt == "e4m3":
        byte = np.frexp(amax)[1] - 1 + 127 - 7
    else:
        mant, ex = np.frexp(amax / 6.0)
        byte = np.where(mant > 0.5, ex, ex - 1) + 127
    byte = np.clip(np.where(amax > 0, byte, 1), 1, 254)
    scaled = (w * np.exp2(127.0 - byte)[:, None, :]).reshape(k, n).astype(np.float32)
    by_word = np.ascontiguousarray(scaled.reshape(k // 512, 128, 4, n).transpose(0, 1, 3, 2))
    if fmt == "e4m3":
        words = by_word.astype(ml_dtypes.float8_e4m3fn).view(np.uint8)
    else:
        c = by_word.astype(ml_dtypes.float4_e2m1fn).view(np.uint8) & 0xF
        words = (c[..., 0::2] | (c[..., 1::2] << 4)).reshape(k // 512, 128, 2 * n)
    return np.ascontiguousarray(words), np.ascontiguousarray(byte.astype(np.uint8).reshape(k // 512, 16, n))


def unpack_weight(words, scales, fmt):
    g, _, n = scales.shape
    words = np.ascontiguousarray(words).reshape(g, 128, n, -1)
    if fmt == "e4m3":
        vals = words.view(ml_dtypes.float8_e4m3fn).astype(np.float64)
    else:
        nib = np.empty((g, 128, n, 4), np.uint8)
        nib[..., 0::2] = words & 0xF
        nib[..., 1::2] = words >> 4
        vals = E2M1[nib]
    vals = vals * np.repeat(np.exp2(scales.astype(np.float64) - 127.0), 8, axis=1)[..., None]
    return vals.transpose(0, 1, 3, 2).reshape(g * 512, n)


def gelu(v):
    return 0.5 * v * (1.0 + np.tanh(np.sqrt(2.0 / np.pi) * (v + 0.044715 * v**3)))


K, T, E1, C1, E2, C2, H = 2048, 1024, 4, 256, 4, 256, 512
N = 512


def deal(E, C):
    slot_token = np.random.permutation(T)
    return slot_token, None, np.random.uniform(0.2, 1.0, T)


def by_expert(wq, xq, E, C):
    return np.concatenate([wq[e].T @ xq[:, e * C:(e + 1) * C] for e in range(E)], axis=1)


def setup_inputs():
    n = np.random.standard_normal
    s = mx_kscale(K)
    u = mx_kscale(H)
    slots1, pos1, g1 = deal(E1, C1)
    slots2, pos2, g2 = deal(E2, C2)
    x = pack_weight(n((K, T)) * s[:, None], "e4m3")
    w2 = [pack_weight(m, "e2m1") for m in n((E2, H, N)) / np.sqrt(H) / u[None, :, None]]
    return {
        "x_words": x[0],
        "x_scales": x[1],
        "w1": (n((E1, K, H)) / np.sqrt(K) / s[None, :, None] * u).astype(np.float32),
        "w2_words": np.stack([m[0] for m in w2]),
        "w2_scales": np.stack([m[1] for m in w2]),
        "gate1": (np.tile(g1, (128, 1))).astype(np.float32),
        "gate2": (np.tile(g2, (128, 1))).astype(np.float32),
        "offs": striped(slots1),
        "offs2": striped(slots2),
    }


def reference(x_words, x_scales, w1, w2_words, w2_scales, gate1, gate2, offs, offs2):
    w1q = mxq(f64(w1), 1, "e4m3")
    w2 = np.stack([unpack_weight(w2_words[e], w2_scales[e], "e2m1") for e in range(E2)])
    idx, idx2 = unstriped(offs), unstriped(offs2)
    xq = unpack_weight(x_words, x_scales, "e4m3")[:, idx]
    h = gelu(by_expert(w1q, xq, E1, C1))
    c = np.zeros((H, T))
    c[:, idx] = f64(gate1[:1]) * h
    y = by_expert(w2, mxq(c[:, idx2], 0, "e4m3"), E2, C2)
    out = np.zeros((N, T))
    out[:, idx2] = f64(gate2[:1]) * y
    return out

@@ -1,0 +1,252 @@
+from contextlib import ExitStack
+
+import concourse.mybir as mybir
+from concourse.masks import make_identity
+
+K, T, H, N = 2048, 1024, 512, 512
+EXPERTS, SLOTS = 4, 256
+FLOPS = 2 * T * K * H + 2 * T * H * N
+
+F32 = mybir.dt.float32
+BF16 = mybir.dt.bfloat16
+I32 = mybir.dt.int32
+U32 = mybir.dt.uint32
+U16 = mybir.dt.uint16
+U8 = mybir.dt.uint8
+FP8X4 = mybir.dt.float8_e4m3fn_x4
+FP4X4 = mybir.dt.float4_e2m1fn_x4
+MULT = mybir.AluOpType.mult
+GELU = mybir.ActivationFunctionType.Gelu_apprx_tanh
+
+P = 128
+PASSES = K // 512
+CHUNKS = EXPERTS * PASSES
+RING = 8
+LIST = 16
+
+
+def vector_columns(n):
+    if n < PASSES:
+        return 0
+    return 192
+
+
+def tile_moe_ser_gelu_kernel(
+    tc, x_words, x_scales, w1, w2_words, w2_scales, gate1, gate2, offs, offs2, out
+):
+    nc = tc.nc
+    with ExitStack() as ctx:
+        keep = ctx.enter_context(tc.tile_pool(name="keep", bufs=1))
+        ring = ctx.enter_context(tc.tile_pool(name="ring", bufs=RING))
+        work = ctx.enter_context(tc.tile_pool(name="work", bufs=2))
+        psum = ctx.enter_context(tc.psum_pool(name="psum", bufs=2))
+
+        list1 = keep.tile([P, T // LIST], U16, name="list1")
+        list2 = keep.tile([P, T // LIST], U16, name="list2")
+        x_word = [keep.tile([P, T], I32, name="x_word%d" % s, align_bytes=64) for s in range(PASSES)]
+        x_scale = keep.tile([P, T], U8, name="x_scale", align_bytes=64)
+        slot_word = [keep.tile([P, T], U32, name="slot_word%d" % s, align_bytes=64) for s in range(PASSES)]
+        slot_scale = keep.tile([P, T], U8, name="slot_scale", align_bytes=64)
+        w2_scale = keep.tile([P, EXPERTS, N], U8, name="w2_scale", align_bytes=64)
+        gate_rows = keep.tile([P, P], F32, name="gate_rows")
+        gate_cols = keep.tile([P, T // P], F32, name="gate_cols")
+        ident = keep.tile([P, P], F32, name="ident")
+        c_pair = [keep.tile([P, T], F32, name="c_pair%d" % u, align_bytes=64) for u in range(2)]
+        y_slot = keep.tile([P, N // P, T], F32, name="y_slot", align_bytes=64)
+        out_tok = [keep.tile([P, T], F32, name="out_tok%d" % b, align_bytes=64) for b in range(N // P)]
+
+        def slots_of(lst, first, count):
+            return lst[:, first // LIST : (first + count) // LIST]
+
+        nc.vector.memset(x_scale[:].bitcast(I32), 0)
+        nc.gpsimd.memset(gate_rows[:], 0.0)
+        nc.gpsimd.memset(w2_scale[:].rearrange("p e n -> p (e n)").bitcast(I32), 0)
+        make_identity(nc, ident[:])
+
+        raw = {}
+
+        def load_w1(n):
+            e, s = divmod(n, PASSES)
+            raw[n] = ring.tile([P, 4, H], F32, name="raw", tag="raw", align_bytes=64)
+            nc.sync.dma_start(out=raw[n][:], in_=w1[e, 512 * s : 512 * (s + 1), :].rearrange("(p j) c -> p j c", j=4))
+
+        def load_x(s):
+            nc.sync.dma_start(out=x_word[s][:], in_=x_words[s].rearrange("p t d -> p (t d)").bitcast(I32))
+
+        nc.sync.dma_start(list1[:], offs)
+        load_x(0)
+        for q in range(4):
+            nc.sync.dma_start(
+                out=x_scale[32 * q : 32 * q + 16, :].bitcast(I32),
+                in_=x_scales[:, 4 * q : 4 * q + 4, :].bitcast(I32),
+            )
+        load_w1(0)
+        for s in range(1, PASSES):
+            load_x(s)
+            load_w1(s)
+        nc.sync.dma_start(out=gate_rows[0 : T // P, :], in_=gate1[0, :].rearrange("(c k) -> c k", k=P))
+        for n in range(PASSES, RING):
+            load_w1(n)
+        nc.sync.dma_start(list2[:], offs2)
+        for q in range(4):
+            nc.sync.dma_start(
+                out=w2_scale[32 * q : 32 * q + 4, :, :].bitcast(I32),
+                in_=w2_scales[:, 0, 4 * q : 4 * q + 4, :].rearrange("e r n -> r e n").bitcast(I32),
+            )
+
+        turned_gate = psum.tile([P, 2, SLOTS], F32, name="turned_gate", tag="turn", bufs=2)
+        nc.tensor.transpose(turned_gate[:, 0, 0:P], gate_rows[:], ident[:])
+        nc.scalar.copy(out=gate_cols[:], in_=turned_gate[:, 0, 0 : T // P])
+
+        late = {}
+
+        def gather_tokens(s):
+            for half in range(2):
+                first = half * (T // 2)
+                nc.vector.tensor_copy(
+                    slot_word[s][:, first : first + T // 2],
+                    x_word[s][:].bitcast(U32).indirect(slots_of(list1, first, T // 2)),
+                )
+
+        def gather_token_scales():
+            for half in range(2):
+                first = half * (T // 2)
+                nc.vector.tensor_copy(
+                    slot_scale[:, first : first + T // 2], x_scale[:].indirect(slots_of(list1, first, T // 2))
+                )
+
+        acc = {}
+        turned = {}
+
+        def activate(e, h):
+            for a in range(2):
+                nc.scalar.activation(
+                    out=h[a].rearrange("p u (m d) -> p u m d", d=2),
+                    in_=acc[e, a][:].rearrange("p (m u d) -> p u m d", u=2, d=2),
+                    func=GELU,
+                )
+                c_row = work.tile([P, 2, SLOTS], BF16, name="c_row", tag="c_row", align_bytes=64)
+                col = 2 * e + a
+                nc.vector.tensor_scalar(c_row[:], h[a], gate_cols[:, col : col + 1], None, MULT)
+                if a == 0 or e == EXPERTS - 1:
+                    bank = psum.tile([P, 2, SLOTS], F32, name="turned", tag="turn", bufs=2)
+                turned[e, a] = bank
+                at = 0 if e == EXPERTS - 1 else a * P
+                for u in range(2):
+                    nc.tensor.transpose(bank[:, u, at : at + P], c_row[:, u, :].bitcast(F32), ident[:])
+
+        def scatter_pairs(e, u, c_slot):
+            nc.scalar.copy(out=c_slot, in_=turned[e, 0][:, u, :])
+            nc.vector.tensor_copy(c_pair[u][:].indirect(slots_of(list1, e * SLOTS, SLOTS)), c_slot)
+
+        for n in range(CHUNKS):
+            e, s = divmod(n, PASSES)
+            grouped = work.tile([P, H, 4], BF16, name="grouped", tag="grouped", bufs=3, align_bytes=64)
+            split = H - vector_columns(n)
+            nc.scalar.copy(
+                out=grouped[:, 0:split, :].rearrange("p (c i) j -> p c j i", i=4),
+                in_=raw[n][:, :, 0:split].rearrange("p j (c i) -> p c j i", i=4),
+            )
+            if split < H:
+                nc.vector.tensor_copy(
+                    out=grouped[:, split:H, :].rearrange("p (c i) j -> p c j i", i=4),
+                    in_=raw[n][:, :, split:H].rearrange("p j (c i) -> p c j i", i=4),
+                )
+            if n + RING < CHUNKS:
+                load_w1(n + RING)
+            elif n + RING == CHUNKS:
+                late["gate2"] = ring.tile([P, T], F32, name="gate2_rows", tag="raw", align_bytes=64)
+                nc.sync.dma_start(out=late["gate2"][:], in_=gate2)
+            elif n + RING == CHUNKS + 1:
+                late["w2"] = ring.tile([P, EXPERTS, 2 * N], U8, name="w2_word", tag="raw", align_bytes=64)
+                nc.sync.dma_start(
+                    out=late["w2"][:].bitcast(I32), in_=w2_words[:, 0, :, :].rearrange("e p n -> p e n").bitcast(I32)
+                )
+            if e == 0:
+                gather_tokens(s)
+                if s == 0:
+                    gather_token_scales()
+
+            w_word = work.tile([P, H], U32, name="w_word", tag="w_word", bufs=4, align_bytes=64)
+            w_scale = work.tile([P, H], U8, name="w_scale", tag="w_scale", bufs=4, align_bytes=64)
+            parts = 2 if split < H else 1
+            for part in range(parts):
+                cols = slice(part * H // parts, (part + 1) * H // parts)
+                nc.vector.quantize_mx(
+                    out=w_word[:, cols].bitcast(FP8X4),
+                    scales=w_scale[:, cols],
+                    in_=grouped[:, cols, :].rearrange("p c j -> p (c j)"),
+                )
+            for a in range(2):
+                if s == 0:
+                    acc[e, a] = psum.tile([P, H], F32, name="acc", tag="acc", bufs=6)
+                cols = slice(e * SLOTS + a * P, e * SLOTS + (a + 1) * P)
+                nc.tensor.matmul_mx(
+                    out=acc[e, a][:],
+                    lhsT=slot_word[s][:, cols].bitcast(FP8X4),
+                    lhsT_scale=slot_scale[4 * s : P, cols],
+                    rhs=w_word[:].bitcast(FP8X4),
+                    rhs_scale=w_scale[:],
+                    start=(s == 0),
+                    stop=(s == PASSES - 1),
+                )
+            if e > 0 and s == 0:
+                activate(e - 1, [raw[n][:, 2 * a : 2 * a + 2, 0:SLOTS] for a in range(2)])
+            if e > 0 and s in (1, 3):
+                scatter_pairs(e - 1, s // 2, raw[n][:, 0, 0:SLOTS])
+
+        last = EXPERTS - 1
+        h_last = work.tile([P, 4, SLOTS], F32, name="h_last", bufs=1, align_bytes=64)
+        activate(last, [h_last[:, 2 * a : 2 * a + 2, :] for a in range(2)])
+        for a in range(2):
+            c_slot = work.tile([P, 2, P], F32, name="c_slot", tag="c_slot", align_bytes=64)
+            nc.scalar.copy(out=c_slot[:], in_=turned[last, a][:, :, 0:P])
+            for u in range(2):
+                nc.vector.tensor_copy(c_pair[u][:].indirect(slots_of(list1, last * SLOTS + a * P, P)), c_slot[:, u, :])
+
+        gate2_rows = late["gate2"]
+        w2_word = late["w2"]
+        for f in range(EXPERTS):
+            got = work.tile([P, 2, SLOTS], U32, name="got", tag="got", bufs=4, align_bytes=64)
+            for u in range(2):
+                nc.vector.tensor_copy(
+                    got[:, u, :], c_pair[u][:].bitcast(U32).indirect(slots_of(list2, f * SLOTS, SLOTS))
+                )
+            woven = work.tile([P, SLOTS, 2], U32, name="woven", tag="woven", bufs=4, align_bytes=64)
+            nc.scalar.copy(out=woven[:], in_=got[:].rearrange("p u m -> p m u"))
+            c_word = work.tile([P, SLOTS], U32, name="c_word", tag="c_word", bufs=4, align_bytes=64)
+            c_scale = work.tile([P, SLOTS], U8, name="c_scale", tag="c_scale", bufs=4, align_bytes=64)
+            nc.vector.quantize_mx(
+                out=c_word[:].bitcast(FP8X4),
+                scales=c_scale[:],
+                in_=woven[:].rearrange("p m u -> p (m u)").bitcast(BF16),
+            )
+            for pair in range(2):
+                y_bank = psum.tile([P, 2, SLOTS], F32, name="y_bank", tag="acc", bufs=6)
+                for i in range(2):
+                    b = 2 * pair + i
+                    nc.tensor.matmul_mx(
+                        out=y_bank[:, i, :],
+                        lhsT=w2_word[:, f, 2 * P * b : 2 * P * (b + 1)].bitcast(FP4X4),
+                        lhsT_scale=w2_scale[:, f, P * b : P * (b + 1)],
+                        rhs=c_word[:].bitcast(FP8X4),
+                        rhs_scale=c_scale[:],
+                        start=True,
+                        stop=True,
+                    )
+                nc.scalar.copy(out=y_slot[:, 2 * pair : 2 * pair + 2, f * SLOTS : (f + 1) * SLOTS], in_=y_bank[:])
+
+        def put_back(b, first, count):
+            nc.vector.tensor_tensor(
+                out_tok[b][:].indirect(slots_of(list2, first, count)),
+                y_slot[:, b, first : first + count],
+                gate2_rows[:, first : first + count],
+                MULT,
+            )
+
+        for f in range(2):
+            for b in range(N // P):
+                put_back(b, f * SLOTS, SLOTS)
+        for b in range(N // P):
+            put_back(b, 2 * SLOTS, 2 * SLOTS)
+            nc.sync.dma_start(out=out[P * b : P * (b + 1), :], in_=out_tok[b][:])

@@ -16,6 +16,7 @@ U8 = mybir.dt.uint8
 FP8X4 = mybir.dt.float8_e4m3fn_x4
 FP4X4 = mybir.dt.float4_e2m1fn_x4
 MULT = mybir.AluOpType.mult
+COPY = mybir.ActivationFunctionType.Copy
 GELU = mybir.ActivationFunctionType.Gelu_apprx_tanh
 
 P = 128
@@ -26,8 +27,10 @@ LIST = 16
 
 
 def vector_columns(n):
-    if n < PASSES:
+    if n < PASSES - 1:
         return 0
+    if n in (PASSES - 1, CHUNKS - 1):
+        return 128
     return 192
 
 
@@ -53,7 +56,6 @@ def tile_moe_ser_gelu_kernel(
         ident = keep.tile([P, P], F32, name="ident")
         c_pair = [keep.tile([P, T], F32, name="c_pair%d" % u, align_bytes=64) for u in range(2)]
         y_slot = keep.tile([P, N // P, T], F32, name="y_slot", align_bytes=64)
-        out_tok = [keep.tile([P, T], F32, name="out_tok%d" % b, align_bytes=64) for b in range(N // P)]
 
         def slots_of(lst, first, count):
             return lst[:, first // LIST : (first + count) // LIST]
@@ -62,6 +64,8 @@ def tile_moe_ser_gelu_kernel(
         nc.gpsimd.memset(gate_rows[:], 0.0)
         nc.gpsimd.memset(w2_scale[:].rearrange("p e n -> p (e n)").bitcast(I32), 0)
         make_identity(nc, ident[:])
+        warm = keep.tile([P, 1], F32, name="warm")
+        nc.scalar.activation(out=warm[:], in_=ident[:, 0:1], func=GELU)
 
         raw = {}
 
@@ -206,21 +210,8 @@ def tile_moe_ser_gelu_kernel(
 
         gate2_rows = late["gate2"]
         w2_word = late["w2"]
-        for f in range(EXPERTS):
-            got = work.tile([P, 2, SLOTS], U32, name="got", tag="got", bufs=4, align_bytes=64)
-            for u in range(2):
-                nc.vector.tensor_copy(
-                    got[:, u, :], c_pair[u][:].bitcast(U32).indirect(slots_of(list2, f * SLOTS, SLOTS))
-                )
-            woven = work.tile([P, SLOTS, 2], U32, name="woven", tag="woven", bufs=4, align_bytes=64)
-            nc.scalar.copy(out=woven[:], in_=got[:].rearrange("p u m -> p m u"))
-            c_word = work.tile([P, SLOTS], U32, name="c_word", tag="c_word", bufs=4, align_bytes=64)
-            c_scale = work.tile([P, SLOTS], U8, name="c_scale", tag="c_scale", bufs=4, align_bytes=64)
-            nc.vector.quantize_mx(
-                out=c_word[:].bitcast(FP8X4),
-                scales=c_scale[:],
-                in_=woven[:].rearrange("p m u -> p (m u)").bitcast(BF16),
-            )
+
+        def second_layer(f, c_word, c_scale):
             for pair in range(2):
                 y_bank = psum.tile([P, 2, SLOTS], F32, name="y_bank", tag="acc", bufs=6)
                 for i in range(2):
@@ -229,12 +220,55 @@ def tile_moe_ser_gelu_kernel(
                         out=y_bank[:, i, :],
                         lhsT=w2_word[:, f, 2 * P * b : 2 * P * (b + 1)].bitcast(FP4X4),
                         lhsT_scale=w2_scale[:, f, P * b : P * (b + 1)],
-                        rhs=c_word[:].bitcast(FP8X4),
-                        rhs_scale=c_scale[:],
+                        rhs=c_word.bitcast(FP8X4),
+                        rhs_scale=c_scale,
                         start=True,
                         stop=True,
                     )
                 nc.scalar.copy(out=y_slot[:, 2 * pair : 2 * pair + 2, f * SLOTS : (f + 1) * SLOTS], in_=y_bank[:])
+
+        def part_pairs(u, tag):
+            c_plane = keep.tile([P, 2, T], BF16, name="c_plane", tag=tag, align_bytes=64)
+            nc.scalar.copy(out=c_plane[:], in_=c_pair[u][:].bitcast(BF16).rearrange("p (t d) -> p d t", d=2))
+            return c_plane
+
+        woven = []
+        for f in range(last):
+            got = work.tile([P, 2, SLOTS], U32, name="got", tag="got", bufs=3, align_bytes=64)
+            for u in range(2):
+                nc.vector.tensor_copy(
+                    got[:, u, :], c_pair[u][:].bitcast(U32).indirect(slots_of(list2, f * SLOTS, SLOTS))
+                )
+            woven.append(work.tile([P, SLOTS, 2], U32, name="woven", tag="woven", bufs=3, align_bytes=64))
+            nc.scalar.copy(out=woven[f][:], in_=got[:].rearrange("p u m -> p m u"))
+        for f in range(last):
+            c_word = keep.tile([P, SLOTS], U32, name="c_word", tag="c_word%d" % f, align_bytes=64)
+            c_scale = work.tile([P, SLOTS], U8, name="c_scale", tag="c_scale", bufs=3, align_bytes=64)
+            nc.vector.quantize_mx(
+                out=c_word[:].bitcast(FP8X4),
+                scales=c_scale[:],
+                in_=woven[f][:].rearrange("p m u -> p (m u)").bitcast(BF16),
+            )
+            second_layer(f, c_word[:], c_scale[:])
+
+        c_plane = [part_pairs(0, "c_plane"), part_pairs(1, "c_word0")]
+        late_first = last * SLOTS
+        c_late = keep.tile([P, SLOTS, 4], BF16, name="c_late", tag="out_last", align_bytes=64)
+        for d in range(4):
+            nc.scalar.activation(
+                out=c_late[:, :, d],
+                in_=c_plane[d // 2][:, d % 2, :].indirect(slots_of(list2, late_first, SLOTS)),
+                func=COPY,
+            )
+        late_word = keep.tile([P, SLOTS], U32, name="late_word", align_bytes=64)
+        late_scale = keep.tile([P, SLOTS], U8, name="late_scale", align_bytes=64)
+        nc.vector.quantize_mx(
+            out=late_word[:].bitcast(FP8X4), scales=late_scale[:], in_=c_late[:].rearrange("p m d -> p (m d)")
+        )
+        second_layer(last, late_word[:], late_scale[:])
+
+        out_tok = [keep.tile([P, T], F32, name="out_tok%d" % b, align_bytes=64) for b in range(N // P - 1)]
+        out_tok.append(keep.tile([P, T], F32, name="out_last", tag="out_last", align_bytes=64))
 
         def put_back(b, first, count):
             nc.vector.tensor_tensor(
@@ -244,9 +278,9 @@ def tile_moe_ser_gelu_kernel(
                 MULT,
             )
 
-        for f in range(2):
+        for first, count in ((0, SLOTS), (SLOTS, 2 * SLOTS)):
             for b in range(N // P):
-                put_back(b, f * SLOTS, SLOTS)
+                put_back(b, first, count)
         for b in range(N // P):
-            put_back(b, 2 * SLOTS, 2 * SLOTS)
+            put_back(b, late_first, SLOTS)
             nc.sync.dma_start(out=out[P * b : P * (b + 1), :], in_=out_tok[b][:])

@@ -16,22 +16,26 @@ U8 = mybir.dt.uint8
 FP8X4 = mybir.dt.float8_e4m3fn_x4
 FP4X4 = mybir.dt.float4_e2m1fn_x4
 MULT = mybir.AluOpType.mult
+ADD = mybir.AluOpType.add
 COPY = mybir.ActivationFunctionType.Copy
 GELU = mybir.ActivationFunctionType.Gelu_apprx_tanh
 
 P = 128
 PASSES = K // 512
 CHUNKS = EXPERTS * PASSES
+HALF = H // 2
 RING = 8
 LIST = 16
 
 
-def vector_columns(n):
+def scalar_columns(n):
     if n < PASSES - 1:
-        return 0
-    if n in (PASSES - 1, CHUNKS - 1):
-        return 128
-    return 192
+        return H
+    if n == PASSES - 1:
+        return 384
+    if n == CHUNKS - 1:
+        return 320
+    return HALF
 
 
 def tile_moe_ser_gelu_kernel(
@@ -143,15 +147,23 @@ def tile_moe_ser_gelu_kernel(
             nc.scalar.copy(out=c_slot, in_=turned[e, 0][:, u, :])
             nc.vector.tensor_copy(c_pair[u][:].indirect(slots_of(list1, e * SLOTS, SLOTS)), c_slot)
 
+        grouped = None
         for n in range(CHUNKS):
             e, s = divmod(n, PASSES)
-            grouped = work.tile([P, H, 4], BF16, name="grouped", tag="grouped", bufs=3, align_bytes=64)
-            split = H - vector_columns(n)
+            before = grouped
+            grouped = work.tile([P, H, 4], BF16, name="grouped", tag="grouped", bufs=4, align_bytes=64)
+            split = scalar_columns(n)
+            after_scatter = n > PASSES and s % 2 == 0
+            upper = before if after_scatter else grouped
             nc.scalar.copy(
                 out=grouped[:, 0:split, :].rearrange("p (c i) j -> p c j i", i=4),
                 in_=raw[n][:, :, 0:split].rearrange("p j (c i) -> p c j i", i=4),
             )
-            if split < H:
+            if after_scatter:
+                nc.gpsimd.tensor_scalar(
+                    upper[:, HALF:H, :], raw[n][:, :, HALF:H].rearrange("p j c -> p c j"), 1.0, 0.0, MULT, ADD
+                )
+            elif split < H:
                 nc.vector.tensor_copy(
                     out=grouped[:, split:H, :].rearrange("p (c i) j -> p c j i", i=4),
                     in_=raw[n][:, :, split:H].rearrange("p j (c i) -> p c j i", i=4),
@@ -179,7 +191,7 @@ def tile_moe_ser_gelu_kernel(
                 nc.vector.quantize_mx(
                     out=w_word[:, cols].bitcast(FP8X4),
                     scales=w_scale[:, cols],
-                    in_=grouped[:, cols, :].rearrange("p c j -> p (c j)"),
+                    in_=(upper if part else grouped)[:, cols, :].rearrange("p c j -> p (c j)"),
                 )
             for a in range(2):
                 if s == 0:

@@ -24,7 +24,7 @@ P = 128
 PASSES = K // 512
 CHUNKS = EXPERTS * PASSES
 HALF = H // 2
-RING = 8
+RING = CHUNKS
 LIST = 16
 
 
@@ -33,8 +33,6 @@ def scalar_columns(n):
         return H
     if n == PASSES - 1:
         return 384
-    if n == CHUNKS - 1:
-        return 320
     return HALF
 
 
@@ -59,7 +57,6 @@ def tile_moe_ser_gelu_kernel(
         gate_cols = keep.tile([P, T // P], F32, name="gate_cols")
         ident = keep.tile([P, P], F32, name="ident")
         c_pair = [keep.tile([P, T], F32, name="c_pair%d" % u, align_bytes=64) for u in range(2)]
-        y_slot = keep.tile([P, N // P, T], F32, name="y_slot", align_bytes=64)
 
         def slots_of(lst, first, count):
             return lst[:, first // LIST : (first + count) // LIST]
@@ -81,8 +78,8 @@ def tile_moe_ser_gelu_kernel(
         def load_x(s):
             nc.sync.dma_start(out=x_word[s][:], in_=x_words[s].rearrange("p t d -> p (t d)").bitcast(I32))
 
-        nc.sync.dma_start(list1[:], offs)
         load_x(0)
+        nc.sync.dma_start(list1[:], offs)
         for q in range(4):
             nc.sync.dma_start(
                 out=x_scale[32 * q : 32 * q + 16, :].bitcast(I32),
@@ -96,17 +93,20 @@ def tile_moe_ser_gelu_kernel(
         for n in range(PASSES, RING):
             load_w1(n)
         nc.sync.dma_start(list2[:], offs2)
+        w2_word = keep.tile([P, EXPERTS, 2 * N], U8, name="w2_word", align_bytes=64)
+        nc.sync.dma_start(out=w2_word[:].bitcast(I32), in_=w2_words[:, 0, :, :].rearrange("e p n -> p e n").bitcast(I32))
         for q in range(4):
             nc.sync.dma_start(
                 out=w2_scale[32 * q : 32 * q + 4, :, :].bitcast(I32),
                 in_=w2_scales[:, 0, 4 * q : 4 * q + 4, :].rearrange("e r n -> r e n").bitcast(I32),
             )
 
+        gate2_rows = keep.tile([P, T], F32, name="gate2_rows", align_bytes=64)
+        nc.sync.dma_start(out=gate2_rows[:], in_=gate2)
+
         turned_gate = psum.tile([P, 2, SLOTS], F32, name="turned_gate", tag="turn", bufs=2)
         nc.tensor.transpose(turned_gate[:, 0, 0:P], gate_rows[:], ident[:])
         nc.scalar.copy(out=gate_cols[:], in_=turned_gate[:, 0, 0 : T // P])
-
-        late = {}
 
         def gather_tokens(s):
             for half in range(2):
@@ -126,25 +126,25 @@ def tile_moe_ser_gelu_kernel(
         acc = {}
         turned = {}
 
-        def activate(e, h):
+        def activate(e, a, h):
+            nc.scalar.activation(
+                out=h.rearrange("p u (m d) -> p u m d", d=2),
+                in_=acc[e, a][:].rearrange("p (m u d) -> p u m d", u=2, d=2),
+                func=GELU,
+            )
+
+        def activate_and_turn(e, h):
+            turned[e] = psum.tile([P, 2, SLOTS], F32, name="turned", tag="turn", bufs=2)
             for a in range(2):
-                nc.scalar.activation(
-                    out=h[a].rearrange("p u (m d) -> p u m d", d=2),
-                    in_=acc[e, a][:].rearrange("p (m u d) -> p u m d", u=2, d=2),
-                    func=GELU,
-                )
+                activate(e, a, h[a])
                 c_row = work.tile([P, 2, SLOTS], BF16, name="c_row", tag="c_row", align_bytes=64)
                 col = 2 * e + a
                 nc.vector.tensor_scalar(c_row[:], h[a], gate_cols[:, col : col + 1], None, MULT)
-                if a == 0 or e == EXPERTS - 1:
-                    bank = psum.tile([P, 2, SLOTS], F32, name="turned", tag="turn", bufs=2)
-                turned[e, a] = bank
-                at = 0 if e == EXPERTS - 1 else a * P
                 for u in range(2):
-                    nc.tensor.transpose(bank[:, u, at : at + P], c_row[:, u, :].bitcast(F32), ident[:])
+                    nc.tensor.transpose(turned[e][:, u, a * P : (a + 1) * P], c_row[:, u, :].bitcast(F32), ident[:])
 
         def scatter_pairs(e, u, c_slot):
-            nc.scalar.copy(out=c_slot, in_=turned[e, 0][:, u, :])
+            nc.scalar.copy(out=c_slot, in_=turned[e][:, u, :])
             nc.vector.tensor_copy(c_pair[u][:].indirect(slots_of(list1, e * SLOTS, SLOTS)), c_slot)
 
         grouped = None
@@ -167,16 +167,6 @@ def tile_moe_ser_gelu_kernel(
                 nc.vector.tensor_copy(
                     out=grouped[:, split:H, :].rearrange("p (c i) j -> p c j i", i=4),
                     in_=raw[n][:, :, split:H].rearrange("p j (c i) -> p c j i", i=4),
-                )
-            if n + RING < CHUNKS:
-                load_w1(n + RING)
-            elif n + RING == CHUNKS:
-                late["gate2"] = ring.tile([P, T], F32, name="gate2_rows", tag="raw", align_bytes=64)
-                nc.sync.dma_start(out=late["gate2"][:], in_=gate2)
-            elif n + RING == CHUNKS + 1:
-                late["w2"] = ring.tile([P, EXPERTS, 2 * N], U8, name="w2_word", tag="raw", align_bytes=64)
-                nc.sync.dma_start(
-                    out=late["w2"][:].bitcast(I32), in_=w2_words[:, 0, :, :].rearrange("e p n -> p e n").bitcast(I32)
                 )
             if e == 0:
                 gather_tokens(s)
@@ -207,21 +197,25 @@ def tile_moe_ser_gelu_kernel(
                     stop=(s == PASSES - 1),
                 )
             if e > 0 and s == 0:
-                activate(e - 1, [raw[n][:, 2 * a : 2 * a + 2, 0:SLOTS] for a in range(2)])
+                activate_and_turn(e - 1, [raw[n][:, 2 * a : 2 * a + 2, 0:SLOTS] for a in range(2)])
             if e > 0 and s in (1, 3):
                 scatter_pairs(e - 1, s // 2, raw[n][:, 0, 0:SLOTS])
 
         last = EXPERTS - 1
         h_last = work.tile([P, 4, SLOTS], F32, name="h_last", bufs=1, align_bytes=64)
-        activate(last, [h_last[:, 2 * a : 2 * a + 2, :] for a in range(2)])
         for a in range(2):
-            c_slot = work.tile([P, 2, P], F32, name="c_slot", tag="c_slot", align_bytes=64)
-            nc.scalar.copy(out=c_slot[:], in_=turned[last, a][:, :, 0:P])
+            activate(last, a, h_last[:, 2 * a : 2 * a + 2, :])
+            col = 2 * last + a
             for u in range(2):
-                nc.vector.tensor_copy(c_pair[u][:].indirect(slots_of(list1, last * SLOTS + a * P, P)), c_slot[:, u, :])
+                c_part = work.tile([P, SLOTS], BF16, name="c_part", tag="c_part", bufs=4, align_bytes=64)
+                nc.vector.tensor_scalar(c_part[:], h_last[:, 2 * a + u, :], gate_cols[:, col : col + 1], None, MULT)
+                bank = psum.tile([P, P], F32, name="bank", tag="turn", bufs=2)
+                nc.tensor.transpose(bank[:], c_part[:].bitcast(F32), ident[:])
+                c_slot = work.tile([P, P], F32, name="c_slot", tag="c_slot", bufs=4, align_bytes=64)
+                nc.scalar.copy(out=c_slot[:], in_=bank[:])
+                nc.vector.tensor_copy(c_pair[u][:].indirect(slots_of(list1, last * SLOTS + a * P, P)), c_slot[:])
 
-        gate2_rows = late["gate2"]
-        w2_word = late["w2"]
+        y_slot = [ring.tile([P, 2, T], F32, name="y_slot", tag="raw", align_bytes=64) for pair in range(2)]
 
         def second_layer(f, c_word, c_scale):
             for pair in range(2):
@@ -237,16 +231,16 @@ def tile_moe_ser_gelu_kernel(
                         start=True,
                         stop=True,
                     )
-                nc.scalar.copy(out=y_slot[:, 2 * pair : 2 * pair + 2, f * SLOTS : (f + 1) * SLOTS], in_=y_bank[:])
+                nc.scalar.copy(out=y_slot[pair][:, :, f * SLOTS : (f + 1) * SLOTS], in_=y_bank[:])
 
-        def part_pairs(u, tag):
-            c_plane = keep.tile([P, 2, T], BF16, name="c_plane", tag=tag, align_bytes=64)
+        def part_pairs(u, pool, tag):
+            c_plane = pool.tile([P, 2, T], BF16, name="c_plane", tag=tag, align_bytes=64)
             nc.scalar.copy(out=c_plane[:], in_=c_pair[u][:].bitcast(BF16).rearrange("p (t d) -> p d t", d=2))
             return c_plane
 
         woven = []
         for f in range(last):
-            got = work.tile([P, 2, SLOTS], U32, name="got", tag="got", bufs=3, align_bytes=64)
+            got = ring.tile([P, 2, SLOTS], U32, name="got", tag="raw", align_bytes=64)
             for u in range(2):
                 nc.vector.tensor_copy(
                     got[:, u, :], c_pair[u][:].bitcast(U32).indirect(slots_of(list2, f * SLOTS, SLOTS))
@@ -263,7 +257,7 @@ def tile_moe_ser_gelu_kernel(
             )
             second_layer(f, c_word[:], c_scale[:])
 
-        c_plane = [part_pairs(0, "c_plane"), part_pairs(1, "c_word0")]
+        c_plane = [part_pairs(0, ring, "raw"), part_pairs(1, keep, "c_word0")]
         late_first = last * SLOTS
         c_late = keep.tile([P, SLOTS, 4], BF16, name="c_late", tag="out_last", align_bytes=64)
         for d in range(4):
@@ -279,13 +273,13 @@ def tile_moe_ser_gelu_kernel(
         )
         second_layer(last, late_word[:], late_scale[:])
 
-        out_tok = [keep.tile([P, T], F32, name="out_tok%d" % b, align_bytes=64) for b in range(N // P - 1)]
+        out_tok = [ring.tile([P, T], F32, name="out_tok", tag="raw", align_bytes=64) for b in range(N // P - 1)]
         out_tok.append(keep.tile([P, T], F32, name="out_last", tag="out_last", align_bytes=64))
 
         def put_back(b, first, count):
             nc.vector.tensor_tensor(
                 out_tok[b][:].indirect(slots_of(list2, first, count)),
-                y_slot[:, b, first : first + count],
+                y_slot[b // 2][:, b % 2, first : first + count],
                 gate2_rows[:, first : first + count],
                 MULT,
             )

from contextlib import ExitStack

import concourse.mybir as mybir
from concourse.masks import make_identity

K, T, H, N = 2048, 1024, 512, 512
EXPERTS, SLOTS = 4, 256
FLOPS = 2 * T * K * H + 2 * T * H * N

F32 = mybir.dt.float32
BF16 = mybir.dt.bfloat16
I32 = mybir.dt.int32
U32 = mybir.dt.uint32
U16 = mybir.dt.uint16
U8 = mybir.dt.uint8
FP8X4 = mybir.dt.float8_e4m3fn_x4
FP4X4 = mybir.dt.float4_e2m1fn_x4
MULT = mybir.AluOpType.mult
ADD = mybir.AluOpType.add
COPY = mybir.ActivationFunctionType.Copy
GELU = mybir.ActivationFunctionType.Gelu_apprx_tanh

P = 128
PASSES = K // 512
CHUNKS = EXPERTS * PASSES
HALF = H // 2
RING = CHUNKS
LIST = 16


def scalar_columns(n):
    if n < PASSES - 1:
        return H
    if n == PASSES - 1:
        return 384
    return HALF


def tile_moe_ser_gelu_kernel(
    tc, x_words, x_scales, w1, w2_words, w2_scales, gate1, gate2, offs, offs2, out
):
    nc = tc.nc
    with ExitStack() as ctx:
        keep = ctx.enter_context(tc.tile_pool(name="keep", bufs=1))
        ring = ctx.enter_context(tc.tile_pool(name="ring", bufs=RING))
        work = ctx.enter_context(tc.tile_pool(name="work", bufs=2))
        psum = ctx.enter_context(tc.psum_pool(name="psum", bufs=2))

        list1 = keep.tile([P, T // LIST], U16, name="list1")
        list2 = keep.tile([P, T // LIST], U16, name="list2")
        x_word = [keep.tile([P, T], I32, name="x_word%d" % s, align_bytes=64) for s in range(PASSES)]
        x_scale = keep.tile([P, T], U8, name="x_scale", align_bytes=64)
        slot_word = [keep.tile([P, T], U32, name="slot_word%d" % s, align_bytes=64) for s in range(PASSES)]
        slot_scale = keep.tile([P, T], U8, name="slot_scale", align_bytes=64)
        w2_scale = keep.tile([P, EXPERTS, N], U8, name="w2_scale", align_bytes=64)
        gate_rows = keep.tile([P, P], F32, name="gate_rows")
        gate_cols = keep.tile([P, T // P], F32, name="gate_cols")
        ident = keep.tile([P, P], F32, name="ident")
        c_pair = [keep.tile([P, T], F32, name="c_pair%d" % u, align_bytes=64) for u in range(2)]

        def slots_of(lst, first, count):
            return lst[:, first // LIST : (first + count) // LIST]

        nc.vector.memset(x_scale[:].bitcast(I32), 0)
        nc.gpsimd.memset(gate_rows[:], 0.0)
        nc.gpsimd.memset(w2_scale[:].rearrange("p e n -> p (e n)").bitcast(I32), 0)
        make_identity(nc, ident[:])
        warm = keep.tile([P, 1], F32, name="warm")
        nc.scalar.activation(out=warm[:], in_=ident[:, 0:1], func=GELU)

        raw = {}

        def load_w1(n):
            e, s = divmod(n, PASSES)
            raw[n] = ring.tile([P, 4, H], F32, name="raw", tag="raw", align_bytes=64)
            nc.sync.dma_start(out=raw[n][:], in_=w1[e, 512 * s : 512 * (s + 1), :].rearrange("(p j) c -> p j c", j=4))

        def load_x(s):
            nc.sync.dma_start(out=x_word[s][:], in_=x_words[s].rearrange("p t d -> p (t d)").bitcast(I32))

        load_x(0)
        nc.sync.dma_start(list1[:], offs)
        for q in range(4):
            nc.sync.dma_start(
                out=x_scale[32 * q : 32 * q + 16, :].bitcast(I32),
                in_=x_scales[:, 4 * q : 4 * q + 4, :].bitcast(I32),
            )
        load_w1(0)
        for s in range(1, PASSES):
            load_x(s)
            load_w1(s)
        nc.sync.dma_start(out=gate_rows[0 : T // P, :], in_=gate1[0, :].rearrange("(c k) -> c k", k=P))
        for n in range(PASSES, RING):
            load_w1(n)
        nc.sync.dma_start(list2[:], offs2)
        w2_word = keep.tile([P, EXPERTS, 2 * N], U8, name="w2_word", align_bytes=64)
        nc.sync.dma_start(out=w2_word[:].bitcast(I32), in_=w2_words[:, 0, :, :].rearrange("e p n -> p e n").bitcast(I32))
        for q in range(4):
            nc.sync.dma_start(
                out=w2_scale[32 * q : 32 * q + 4, :, :].bitcast(I32),
                in_=w2_scales[:, 0, 4 * q : 4 * q + 4, :].rearrange("e r n -> r e n").bitcast(I32),
            )

        gate2_rows = keep.tile([P, T], F32, name="gate2_rows", align_bytes=64)
        nc.sync.dma_start(out=gate2_rows[:], in_=gate2)

        turned_gate = psum.tile([P, 2, SLOTS], F32, name="turned_gate", tag="turn", bufs=2)
        nc.tensor.transpose(turned_gate[:, 0, 0:P], gate_rows[:], ident[:])
        nc.scalar.copy(out=gate_cols[:], in_=turned_gate[:, 0, 0 : T // P])

        def gather_tokens(s):
            for half in range(2):
                first = half * (T // 2)
                nc.vector.tensor_copy(
                    slot_word[s][:, first : first + T // 2],
                    x_word[s][:].bitcast(U32).indirect(slots_of(list1, first, T // 2)),
                )

        def gather_token_scales():
            for half in range(2):
                first = half * (T // 2)
                nc.vector.tensor_copy(
                    slot_scale[:, first : first + T // 2], x_scale[:].indirect(slots_of(list1, first, T // 2))
                )

        acc = {}
        turned = {}

        def activate(e, a, h):
            nc.scalar.activation(
                out=h.rearrange("p u (m d) -> p u m d", d=2),
                in_=acc[e, a][:].rearrange("p (m u d) -> p u m d", u=2, d=2),
                func=GELU,
            )

        def activate_and_turn(e, h):
            turned[e] = psum.tile([P, 2, SLOTS], F32, name="turned", tag="turn", bufs=2)
            for a in range(2):
                activate(e, a, h[a])
                c_row = work.tile([P, 2, SLOTS], BF16, name="c_row", tag="c_row", align_bytes=64)
                col = 2 * e + a
                nc.vector.tensor_scalar(c_row[:], h[a], gate_cols[:, col : col + 1], None, MULT)
                for u in range(2):
                    nc.tensor.transpose(turned[e][:, u, a * P : (a + 1) * P], c_row[:, u, :].bitcast(F32), ident[:])

        def scatter_pairs(e, u, c_slot):
            nc.scalar.copy(out=c_slot, in_=turned[e][:, u, :])
            nc.vector.tensor_copy(c_pair[u][:].indirect(slots_of(list1, e * SLOTS, SLOTS)), c_slot)

        grouped = None
        for n in range(CHUNKS):
            e, s = divmod(n, PASSES)
            before = grouped
            grouped = work.tile([P, H, 4], BF16, name="grouped", tag="grouped", bufs=4, align_bytes=64)
            split = scalar_columns(n)
            after_scatter = n > PASSES and s % 2 == 0
            upper = before if after_scatter else grouped
            nc.scalar.copy(
                out=grouped[:, 0:split, :].rearrange("p (c i) j -> p c j i", i=4),
                in_=raw[n][:, :, 0:split].rearrange("p j (c i) -> p c j i", i=4),
            )
            if after_scatter:
                nc.gpsimd.tensor_scalar(
                    upper[:, HALF:H, :], raw[n][:, :, HALF:H].rearrange("p j c -> p c j"), 1.0, 0.0, MULT, ADD
                )
            elif split < H:
                nc.vector.tensor_copy(
                    out=grouped[:, split:H, :].rearrange("p (c i) j -> p c j i", i=4),
                    in_=raw[n][:, :, split:H].rearrange("p j (c i) -> p c j i", i=4),
                )
            if e == 0:
                gather_tokens(s)
                if s == 0:
                    gather_token_scales()

            w_word = work.tile([P, H], U32, name="w_word", tag="w_word", bufs=4, align_bytes=64)
            w_scale = work.tile([P, H], U8, name="w_scale", tag="w_scale", bufs=4, align_bytes=64)
            parts = 2 if split < H else 1
            for part in range(parts):
                cols = slice(part * H // parts, (part + 1) * H // parts)
                nc.vector.quantize_mx(
                    out=w_word[:, cols].bitcast(FP8X4),
                    scales=w_scale[:, cols],
                    in_=(upper if part else grouped)[:, cols, :].rearrange("p c j -> p (c j)"),
                )
            for a in range(2):
                if s == 0:
                    acc[e, a] = psum.tile([P, H], F32, name="acc", tag="acc", bufs=6)
                cols = slice(e * SLOTS + a * P, e * SLOTS + (a + 1) * P)
                nc.tensor.matmul_mx(
                    out=acc[e, a][:],
                    lhsT=slot_word[s][:, cols].bitcast(FP8X4),
                    lhsT_scale=slot_scale[4 * s : P, cols],
                    rhs=w_word[:].bitcast(FP8X4),
                    rhs_scale=w_scale[:],
                    start=(s == 0),
                    stop=(s == PASSES - 1),
                )
            if e > 0 and s == 0:
                activate_and_turn(e - 1, [raw[n][:, 2 * a : 2 * a + 2, 0:SLOTS] for a in range(2)])
            if e > 0 and s in (1, 3):
                scatter_pairs(e - 1, s // 2, raw[n][:, 0, 0:SLOTS])

        last = EXPERTS - 1
        h_last = work.tile([P, 4, SLOTS], F32, name="h_last", bufs=1, align_bytes=64)
        for a in range(2):
            activate(last, a, h_last[:, 2 * a : 2 * a + 2, :])
            col = 2 * last + a
            for u in range(2):
                c_part = work.tile([P, SLOTS], BF16, name="c_part", tag="c_part", bufs=4, align_bytes=64)
                nc.vector.tensor_scalar(c_part[:], h_last[:, 2 * a + u, :], gate_cols[:, col : col + 1], None, MULT)
                bank = psum.tile([P, P], F32, name="bank", tag="turn", bufs=2)
                nc.tensor.transpose(bank[:], c_part[:].bitcast(F32), ident[:])
                c_slot = work.tile([P, P], F32, name="c_slot", tag="c_slot", bufs=4, align_bytes=64)
                nc.scalar.copy(out=c_slot[:], in_=bank[:])
                nc.vector.tensor_copy(c_pair[u][:].indirect(slots_of(list1, last * SLOTS + a * P, P)), c_slot[:])

        y_slot = [ring.tile([P, 2, T], F32, name="y_slot", tag="raw", align_bytes=64) for pair in range(2)]

        def second_layer(f, c_word, c_scale):
            for pair in range(2):
                y_bank = psum.tile([P, 2, SLOTS], F32, name="y_bank", tag="acc", bufs=6)
                for i in range(2):
                    b = 2 * pair + i
                    nc.tensor.matmul_mx(
                        out=y_bank[:, i, :],
                        lhsT=w2_word[:, f, 2 * P * b : 2 * P * (b + 1)].bitcast(FP4X4),
                        lhsT_scale=w2_scale[:, f, P * b : P * (b + 1)],
                        rhs=c_word.bitcast(FP8X4),
                        rhs_scale=c_scale,
                        start=True,
                        stop=True,
                    )
                nc.scalar.copy(out=y_slot[pair][:, :, f * SLOTS : (f + 1) * SLOTS], in_=y_bank[:])

        def part_pairs(u, pool, tag):
            c_plane = pool.tile([P, 2, T], BF16, name="c_plane", tag=tag, align_bytes=64)
            nc.scalar.copy(out=c_plane[:], in_=c_pair[u][:].bitcast(BF16).rearrange("p (t d) -> p d t", d=2))
            return c_plane

        woven = []
        for f in range(last):
            got = ring.tile([P, 2, SLOTS], U32, name="got", tag="raw", align_bytes=64)
            for u in range(2):
                nc.vector.tensor_copy(
                    got[:, u, :], c_pair[u][:].bitcast(U32).indirect(slots_of(list2, f * SLOTS, SLOTS))
                )
            woven.append(work.tile([P, SLOTS, 2], U32, name="woven", tag="woven", bufs=3, align_bytes=64))
            nc.scalar.copy(out=woven[f][:], in_=got[:].rearrange("p u m -> p m u"))
        for f in range(last):
            c_word = keep.tile([P, SLOTS], U32, name="c_word", tag="c_word%d" % f, align_bytes=64)
            c_scale = work.tile([P, SLOTS], U8, name="c_scale", tag="c_scale", bufs=3, align_bytes=64)
            nc.vector.quantize_mx(
                out=c_word[:].bitcast(FP8X4),
                scales=c_scale[:],
                in_=woven[f][:].rearrange("p m u -> p (m u)").bitcast(BF16),
            )
            second_layer(f, c_word[:], c_scale[:])

        c_plane = [part_pairs(0, ring, "raw"), part_pairs(1, keep, "c_word0")]
        late_first = last * SLOTS
        c_late = keep.tile([P, SLOTS, 4], BF16, name="c_late", tag="out_last", align_bytes=64)
        for d in range(4):
            nc.scalar.activation(
                out=c_late[:, :, d],
                in_=c_plane[d // 2][:, d % 2, :].indirect(slots_of(list2, late_first, SLOTS)),
                func=COPY,
            )
        late_word = keep.tile([P, SLOTS], U32, name="late_word", align_bytes=64)
        late_scale = keep.tile([P, SLOTS], U8, name="late_scale", align_bytes=64)
        nc.vector.quantize_mx(
            out=late_word[:].bitcast(FP8X4), scales=late_scale[:], in_=c_late[:].rearrange("p m d -> p (m d)")
        )
        second_layer(last, late_word[:], late_scale[:])

        out_tok = [ring.tile([P, T], F32, name="out_tok", tag="raw", align_bytes=64) for b in range(N // P - 1)]
        out_tok.append(keep.tile([P, T], F32, name="out_last", tag="out_last", align_bytes=64))

        def put_back(b, first, count):
            nc.vector.tensor_tensor(
                out_tok[b][:].indirect(slots_of(list2, first, count)),
                y_slot[b // 2][:, b % 2, first : first + count],
                gate2_rows[:, first : first + count],
                MULT,
            )

        for first, count in ((0, SLOTS), (SLOTS, 2 * SLOTS)):
            for b in range(N // P):
                put_back(b, first, count)
        for b in range(N // P):
            put_back(b, late_first, SLOTS)
            nc.sync.dma_start(out=out[P * b : P * (b + 1), :], in_=out_tok[b][:])
